import numpy as np
import ml_dtypes


def mxq(x, axis, fmt="e4m3"):
    dtype, down = {"e4m3": (ml_dtypes.float8_e4m3fn, 7), "e5m2": (ml_dtypes.float8_e5m2, 14)}[fmt]
    v = np.moveaxis(np.asarray(x, np.float32).astype(ml_dtypes.bfloat16).astype(np.float64), axis, -1)
    blocks = v.reshape(v.shape[:-1] + (-1, 32))
    amax = np.abs(blocks).max(-1, keepdims=True)
    byte = np.maximum(np.where(amax > 0, np.frexp(amax)[1] - 1 + 127, 0) - down, 1)
    scale = np.exp2(byte - 127.0)
    codes = (blocks / scale).astype(np.float32).astype(dtype).astype(np.float64)
    return np.moveaxis((codes * scale).reshape(v.shape), -1, axis)


WIDE = False


def mx_kscale(k):
    if not WIDE:
        return np.ones(k)
    levels = np.array([10, -10, 5, -5, 0])
    if k % 512:
        return np.exp2(np.random.permutation(np.resize(levels, k // 32))).repeat(32)
    a = np.empty((k // 512, 16))
    for p in range(k // 512):
        a[p, :8] = np.random.permutation(np.resize(levels, 8))
        for g in range(8):
            far = levels[np.abs(levels - a[p, g]) >= 10]
            a[p, g + 8] = far[np.random.randint(len(far))]
    return np.exp2(a.ravel()).repeat(32)


BF16 = ml_dtypes.bfloat16


def bf(x):
    return np.asarray(x, np.float32).astype(BF16)


def f64(x):
    return np.asarray(x).astype(np.float64)


E2M1 = np.array([0.0, 0.5, 1.0, 1.5, 2.0, 3.0, 4.0, 6.0, -0.0, -0.5, -1.0, -1.5, -2.0, -3.0, -4.0, -6.0])


def pack_weight(w, fmt):
    k, n = w.shape
    w = f64(bf(w)).reshape(k // 32, 32, n)
    amax = np.abs(w).max(1)
    if fmt == "e4m3":
        byte = np.frexp(amax)[1] - 1 + 127 - 7
    else:
        mant, ex = np.frexp(amax / 6.0)
        byte = np.where(mant > 0.5, ex, ex - 1) + 127
    byte = np.clip(np.where(amax > 0, byte, 1), 1, 254)
    scaled = (w * np.exp2(127.0 - byte)[:, None, :]).reshape(k, n).astype(np.float32)
    by_word = np.ascontiguousarray(scaled.reshape(k // 512, 128, 4, n).transpose(0, 1, 3, 2))
    if fmt == "e4m3":
        words = by_word.astype(ml_dtypes.float8_e4m3fn).view(np.uint8)
    else:
        c = by_word.astype(ml_dtypes.float4_e2m1fn).view(np.uint8) & 0xF
        words = c[..., 0::2] | (c[..., 1::2] << 4)
    return np.ascontiguousarray(words), np.ascontiguousarray(byte.astype(np.uint8).reshape(k // 512, 16, n))


def unpack_weight(words, scales, fmt):
    g, p, n, _ = words.shape
    if fmt == "e4m3":
        vals = np.ascontiguousarray(words).view(ml_dtypes.float8_e4m3fn).astype(np.float64)
    else:
        nib = np.empty((g, p, n, 4), np.uint8)
        nib[..., 0::2] = words & 0xF
        nib[..., 1::2] = words >> 4
        vals = E2M1[nib]
    vals = vals * np.repeat(np.exp2(scales.astype(np.float64) - 127.0), 8, axis=1)[..., None]
    return vals.transpose(0, 1, 3, 2).reshape(g * 512, n)
def pack4(w):
    words, scales = pack_weight(w, "e2m1")
    return words.reshape(words.shape[0], 128, -1), scales


def unpack4(words, scales):
    return unpack_weight(words.reshape(words.shape[0], 128, -1, 2), scales, "e2m1")


def planes(Y):
    n, m = Y.shape
    b = f64(bf(Y)).reshape(n // 32, 32, m)
    amax = np.abs(b).max(1)
    byte = np.clip(np.where(amax > 0, np.frexp(amax)[1] - 1 + 127 - 7, 1), 1, 254)
    codes = (b * np.exp2(127.0 - byte)[:, None, :]).reshape(n, m).astype(np.float32).astype(ml_dtypes.float8_e4m3fn).view(np.uint8)
    words = codes.reshape(n // 512, 128, 4, m).transpose(0, 1, 3, 2)
    return np.ascontiguousarray(words), np.ascontiguousarray(byte.astype(np.uint8).reshape(n // 512, 16, m))


G, R, E, S = 4, 512, 512, 1024
COEF = [-2.0, -1.0, -1.0, 0.0, 0.0, 0.0, 0.0, 1.0, 1.0, 2.0]

def setup_inputs():
    s = mx_kscale(G * E)
    t = mx_kscale(G * S)
    A = np.random.choice(COEF, size=(G, E, S))
    lam = 0.6 * np.random.randn(G, R, E) / np.sqrt(E) / s.reshape(G, 1, E)
    kform = 5.0 * np.exp(0.3 * np.random.randn(G, S)) / np.sqrt(S) * t.reshape(G, S)
    f_words, f_scales = pack4(A.reshape(G * E, S) * s[:, None])
    h_words, h_scales = pack4(A.swapaxes(1, 2).reshape(G * S, E) / t[:, None])
    return {
        "lam": bf(lam),
        "f_words": f_words,
        "f_scales": f_scales,
        "kform": bf(kform),
        "h_words": h_words,
        "h_scales": h_scales,
        "vol": bf(0.2 * np.exp(0.3 * np.random.randn(G, R))),
        "total": bf(np.random.randn(G, R, E)),
        "mass": bf(np.exp(0.8 * np.random.randn(E))),
    }

def reference(lam, f_words, f_scales, kform, h_words, h_scales, vol, total, mass):
    F = unpack4(f_words, f_scales).reshape(G, E, S)
    H = unpack4(h_words, h_scales).reshape(G, S, E)
    z = mxq(f64(lam), 2) @ F
    conc = np.exp(z) * f64(kform)[:, None, :]
    b = mxq(conc, 2) @ H
    y = (f64(total) - f64(vol)[:, :, None] * b) * f64(mass)
    Y = y.reshape(G * R, E).T
    words, scales = planes(Y)
    return y, words, scales

@@ -1,0 +1,423 @@
+from contextlib import ExitStack
+
+import concourse.mybir as mybir
+from concourse.masks import make_identity
+
+G, R, E, S = 4, 512, 512, 1024
+FLOPS = 2 * 2 * G * R * E * S
+
+F32 = mybir.dt.float32
+BF16 = mybir.dt.bfloat16
+I32 = mybir.dt.int32
+U32 = mybir.dt.uint32
+U8 = mybir.dt.uint8
+FP8X4 = mybir.dt.float8_e4m3fn_x4
+FP4X4 = mybir.dt.float4_e2m1fn_x4
+ACT = mybir.ActivationFunctionType
+ALU = mybir.AluOpType
+
+P = 128
+PACK = 4
+KP = P * PACK
+CELLS = 256
+TILES = CELLS // P
+UNITS = G * R // CELLS
+PER_SYS = R // CELLS
+GROUPS = S // KP
+FRONT = [(0, j, 1) for j in range(TILES)] + [(u, 0, TILES) for u in range(1, UNITS)]
+
+
+def tile_grouped_mass_action_balance_k7_kernel(
+    tc, lam, f_words, f_scales, kform, h_words, h_scales, vol, total, mass, out_0, out_1, out_2
+):
+    nc = tc.nc
+    with ExitStack() as ctx:
+        keep = ctx.enter_context(tc.tile_pool(name="keep", bufs=1))
+        work = ctx.enter_context(tc.tile_pool(name="work", bufs=2))
+        psum = ctx.enter_context(tc.psum_pool(name="psum", bufs=1))
+        ctx.enter_context(tc.manual_schedule())
+
+        def rows_of(x, u):
+            c, h = divmod(u, PER_SYS)
+            return x[c, h * CELLS : (h + 1) * CELLS, :].rearrange("(p j) i -> p j i", j=TILES)
+
+        lam_sb = [keep.tile([P, TILES, E], BF16, name="lam%d" % u) for u in range(UNITS)]
+        tot_sb = [keep.tile([P, TILES, E], BF16, name="tot%d" % u) for u in range(UNITS)]
+        f_raw = [keep.tile([P, 2 * S], U8, name="fraw%d" % c) for c in range(G)]
+        f_perm = [keep.tile([P, 2 * S], U8, name="fperm%d" % c, align_bytes=64) for c in range(G)]
+        fs_raw = keep.tile([P, G, S], U8)
+        fs_perm = [keep.tile([P, S], U8, name="fsperm%d" % c, align_bytes=64) for c in range(G)]
+        h_sb = [keep.tile([P, GROUPS, 2 * E], U8, name="h%d" % c, align_bytes=64) for c in range(G)]
+        hs_sb = keep.tile([P, G * GROUPS, E], U8, align_bytes=64)
+        k_sb = keep.tile([P, P], BF16)
+        k_rows = keep.tile([P, P], BF16)
+        vol_sb = keep.tile([P, UNITS, TILES], BF16)
+        neg_vol = keep.tile([P, UNITS * TILES], F32)
+        mass_sb = keep.tile([P, E], BF16)
+        ident = keep.tile([P, P], F32)
+        ident_bf = keep.tile([P, P], BF16)
+        warm = keep.tile([P, 1], F32)
+        y_codes = keep.tile([P, G * R], U32, align_bytes=64)
+        y_scales = keep.tile([P, G * R], U8, align_bytes=64)
+        consts = psum.tile([P, PACK + 1, P], BF16, tag="consts")
+        k_ps = consts[:, PACK, :]
+        mass4 = keep.tile([P, PACK], BF16)
+
+        nc.vector.memset(warm[:], 0.0)
+        nc.vector.memset(fs_raw[:, 0, :].bitcast(I32), 0)
+        make_identity(nc, ident[:])
+        nc.scalar.activation(warm[:], warm[:], ACT.Exp)
+        nc.vector.memset(k_sb[:], 0.0)
+        nc.vector.memset(fs_raw[:, 1:G, :].rearrange("p c n -> p (c n)").bitcast(I32), 0)
+        nc.gpsimd.memset(hs_sb[:].rearrange("p c n -> p (c n)").bitcast(I32), 0)
+
+        def load_lam(u):
+            nc.sync.dma_start(out=lam_sb[u][:], in_=rows_of(lam, u))
+
+        def load_total(u):
+            nc.sync.dma_start(out=tot_sb[u][:], in_=rows_of(total, u))
+
+        def load_f(c, lo=0, hi=2 * S):
+            nc.sync.dma_start(out=f_raw[c][:, lo:hi].bitcast(I32), in_=f_words[c][:, lo:hi].bitcast(I32))
+
+        def load_h(c):
+            src = h_words[GROUPS * c : GROUPS * (c + 1)].rearrange("g p n -> p g n")
+            nc.sync.dma_start(out=h_sb[c][:].bitcast(I32), in_=src.bitcast(I32))
+
+        def load_scales(dst, src, lo, hi):
+            for q in range(4):
+                rows = src[lo:hi, 4 * q : 4 * q + 4, :].rearrange("g r n -> r g n")
+                nc.sync.dma_start(out=dst[32 * q : 32 * q + 4, lo:hi].bitcast(I32), in_=rows.bitcast(I32))
+
+        nc.sync.dma_start(out=lam_sb[0][:, 0, :], in_=rows_of(lam, 0)[:, 0, :])
+        load_f(0, 0, S)
+        load_scales(fs_raw, f_scales, 0, 1)
+        nc.sync.dma_start(out=lam_sb[0][:, 1, :], in_=rows_of(lam, 0)[:, 1, :])
+        load_f(0, S, 2 * S)
+        k_src = kform.rearrange("c (g p t) -> p (c g) t", g=GROUPS, t=PACK)
+        nc.sync.dma_start(out=k_sb[:, 0 : PACK * G * GROUPS].rearrange("p (x t) -> p x t", t=PACK), in_=k_src)
+        load_lam(1)
+        load_f(1)
+        load_lam(2)
+        load_scales(fs_raw, f_scales, 1, G)
+        nc.sync.dma_start(out=mass4[:], in_=mass.rearrange("(p t) -> p t", t=PACK))
+        load_scales(hs_sb, h_scales, 0, GROUPS)
+        load_h(0)
+        load_f(2)
+        load_lam(3)
+        load_total(0)
+        nc.sync.dma_start(out=vol_sb[:], in_=vol.rearrange("c (h p j) -> p (c h) j", p=P, j=TILES))
+        nc.sync.dma_start(out=mass_sb[:], in_=mass.partition_broadcast(P))
+        load_f(3)
+        load_lam(4)
+        load_total(1)
+        load_scales(hs_sb, h_scales, GROUPS, G * GROUPS)
+        for u in range(2, UNITS):
+            if u % PER_SYS == 0:
+                load_h(u // PER_SYS)
+            if u + 3 < UNITS:
+                load_lam(u + 3)
+            load_total(u)
+        nc.gpsimd.tensor_scalar(neg_vol[:], vol_sb[:].rearrange("p u j -> p (u j)"), -1.0, 0.0, ALU.mult, ALU.add)
+
+        t = {}
+
+        def live(u):
+            return 0 <= u < UNITS
+
+        def permute_codes(c, g):
+            w = slice(2 * KP * g, 2 * KP * (g + 1))
+            nc.vector.tensor_copy(
+                f_perm[c][:, w].rearrange("p (t m b) -> p t m b", t=PACK, b=2),
+                f_raw[c][:, w].rearrange("p (m t b) -> p t m b", t=PACK, b=2),
+            )
+
+        def permute_scales(c, g):
+            s = slice(KP * g, KP * (g + 1))
+            nc.vector.tensor_copy(
+                fs_perm[c][:, s].rearrange("p (t m) -> p t m", t=PACK),
+                fs_raw[:, c, s].rearrange("p (m t) -> p t m", t=PACK),
+            )
+
+        def permute_f(c, g):
+            permute_codes(c, g)
+            permute_scales(c, g)
+
+        def turn_lam(f):
+            u, j0, n = FRONT[f]
+            bank = psum.tile([P, n * 2, P], F32, tag=("turn_y" if f == 1 else "turn_lam"), name="lam_bank")
+            t["lam_bank", f] = bank
+            for j in range(n):
+                words = lam_sb[u][:, j0 + j, :].bitcast(F32)
+                for w in range(2):
+                    nc.tensor.transpose(bank[:, 2 * j + w, :], words[:, w : E // 2 : 2], ident[:])
+
+        def lay_lam(f):
+            n = FRONT[f][2]
+            lam_t = work.tile([P, n * KP], BF16, tag="lam_t", name="lam_t", align_bytes=64)
+            t["lam_t", f] = lam_t
+            nc.scalar.copy(
+                lam_t[:].bitcast(F32).rearrange("p (j r w) -> p j r w", j=n, w=2),
+                t["lam_bank", f][:].rearrange("p (j w) r -> p j r w", w=2),
+            )
+
+        def quantise_lam(f):
+            n = FRONT[f][2]
+            codes = work.tile([P, n * P], U32, tag="lam_codes", name="lam_codes", bufs=3, align_bytes=64)
+            scales = work.tile([P, n * P], U8, tag="lam_scales", name="lam_scales", bufs=3, align_bytes=64)
+            t["lam_q", f] = (codes, scales)
+            nc.vector.quantize_mx(out=codes[:].bitcast(FP8X4), scales=scales[:], in_=t["lam_t", f][:])
+
+        def mm_z(f, g, a):
+            u, j0, n = FRONT[f]
+            if a >= n:
+                return
+            c = u // PER_SYS
+            side = PACK // n
+            codes, scales = t["lam_q", f]
+            bank = psum.tile([P, side, n * P], F32, tag="z", name="z_bank", bufs=3)
+            t["z", f, g, a] = bank
+            for e in range(side):
+                col = KP * g + P * (side * a + e)
+                nc.tensor.matmul_mx(
+                    out=bank[:, e, :],
+                    lhsT=f_perm[c][:, 2 * col : 2 * (col + P)].bitcast(FP4X4),
+                    lhsT_scale=fs_perm[c][:, col : col + P],
+                    rhs=codes[:].bitcast(FP8X4),
+                    rhs_scale=scales[:],
+                    start=True,
+                    stop=True,
+                )
+
+        def exp_z(f, g, a):
+            n = FRONT[f][2]
+            if a >= n:
+                return
+            if a == 0:
+                t["ex", f, g] = work.tile([P, n, n * P, PACK // n], F32, tag="ex", name="ex", bufs=4)
+            nc.scalar.activation(t["ex", f, g][:, a], t["z", f, g, a][:].rearrange("p e n -> p n e"), ACT.Exp)
+
+        def times_k(f, g):
+            u, j0, n = FRONT[f]
+            conc = work.tile([P, n * KP], BF16, tag="conc", name="conc", bufs=3, align_bytes=64)
+            t["conc", f, g] = conc
+            k0 = PACK * (GROUPS * (u // PER_SYS) + g)
+            k_view = (k_sb if f < 2 else k_ps)[:, k0 : k0 + PACK].rearrange("p (a e) -> p a e", a=n).unsqueeze(1)
+            nc.vector.tensor_tensor(
+                conc[:].rearrange("p (n a e) -> p n a e", a=n, e=PACK // n),
+                t["ex", f, g][:].rearrange("p a n e -> p n a e"),
+                k_view.to_broadcast([P, n * P, n, PACK // n]),
+                ALU.mult,
+            )
+
+        def quantise_conc(f, g):
+            u, j0, n = FRONT[f]
+            codes = work.tile([P, n * P], U32, tag="conc_codes", name="conc_codes", bufs=6, align_bytes=64)
+            scales = work.tile([P, n * P], U8, tag="conc_scales", name="conc_scales", bufs=6, align_bytes=64)
+            for j in range(n):
+                t["conc_q", u, j0 + j, g] = (codes[:, P * j : P * (j + 1)], scales[:, P * j : P * (j + 1)])
+            nc.vector.quantize_mx(out=codes[:].bitcast(FP8X4), scales=scales[:], in_=t["conc", f, g][:])
+
+        def mm_b(u, j):
+            c = u // PER_SYS
+            bank = psum.tile([P, E], F32, tag="b", name="b_bank", bufs=2)
+            t["b", u, j] = bank
+            for g in range(GROUPS):
+                codes, scales = t["conc_q", u, j, g]
+                nc.tensor.matmul_mx(
+                    out=bank[:],
+                    lhsT=codes.bitcast(FP8X4),
+                    lhsT_scale=scales,
+                    rhs=h_sb[c][:, g, :].bitcast(FP4X4),
+                    rhs_scale=hs_sb[:, GROUPS * c + g, :],
+                    start=(g == 0),
+                    stop=(g == GROUPS - 1),
+                )
+
+        def turn_k():
+            bank = psum.tile([P, P], BF16, tag="turn_y", name="k_bank")
+            nc.tensor.transpose(bank[:], k_sb[:], ident_bf[:])
+            t["k_bank"] = bank
+
+        def spread_constants():
+            nc.tensor.transpose(k_ps, k_rows[:], ident_bf[:])
+            for e in range(PACK):
+                nc.tensor.transpose(consts[:, e, :], mass4[:, e : e + 1].to_broadcast([P, P]), ident_bf[:])
+
+        def balance(u, j):
+            res = work.tile([P, E], F32, tag="res", name="res", bufs=4)
+            t["res", u, j] = res
+            col = TILES * u + j
+            nc.vector.scalar_tensor_tensor(
+                res[:], t["b", u, j][:], neg_vol[:, col : col + 1], tot_sb[u][:, j, :], ALU.mult, ALU.add
+            )
+
+        def times_mass(u, j):
+            y = work.tile([P, E], F32, tag="y", name="y", bufs=6)
+            t["y", u, j] = y
+            nc.gpsimd.tensor_tensor(y[:], t["res", u, j][:], mass_sb[:], ALU.mult)
+            nc.sync.dma_start(out=rows_of(out_0, u)[:, j, :], in_=y[:])
+
+        def times_mass_v(u, j):
+            y = work.tile([P, E], F32, tag="y", name="y", bufs=6)
+            t["y", u, j] = y
+            nc.vector.tensor_tensor(
+                y[:].rearrange("r (q e) -> r q e", e=PACK),
+                t["res", u, j][:].rearrange("r (q e) -> r q e", e=PACK),
+                consts[:, 0:PACK, :].rearrange("r e q -> r q e"),
+                ALU.mult,
+            )
+            nc.sync.dma_start(out=rows_of(out_0, u)[:, j, :], in_=y[:])
+
+        def round_y(u, j):
+            y_bf = work.tile([P, E], BF16, tag="y_bf", name="y_bf", bufs=4)
+            t["y_bf", u, j] = y_bf
+            dst = y_bf[:].rearrange("r (w q e) -> r w q e", w=2, e=2)
+            nc.scalar.copy(dst, t["y", u, j][:].rearrange("r (q w e) -> r w q e", w=2, e=2))
+
+        def round_y_v(u, j):
+            y_bf = work.tile([P, E], BF16, tag="y_bf", name="y_bf", bufs=4)
+            t["y_bf", u, j] = y_bf
+            nc.vector.tensor_tensor(
+                y_bf[:].rearrange("r (w q e) -> r w q e", w=2, e=2),
+                t["res", u, j][:].rearrange("r (q w e) -> r w q e", w=2, e=2),
+                consts[:, 0:PACK, :].rearrange("r (w e) q -> r w q e", w=2),
+                ALU.mult,
+            )
+
+        def turn_y(u, j):
+            if j == 0:
+                t["y_bank", u] = psum.tile([P, TILES * 2, P], F32, tag=("turn_lam" if u == UNITS - 1 else "turn_y"), name="y_bank")
+            words = t["y_bf", u, j][:].bitcast(F32)
+            for w in range(2):
+                nc.tensor.transpose(t["y_bank", u][:, 2 * j + w, :], words[:, P * w : P * (w + 1)], ident[:])
+
+        def lay_y(u):
+            y_t = work.tile([P, CELLS * PACK], BF16, tag="y_t", name="y_t", align_bytes=64)
+            t["y_t", u] = y_t
+            nc.scalar.copy(
+                y_t[:].bitcast(F32).rearrange("p (r j w) -> p r j w", j=TILES, w=2),
+                t["y_bank", u][:].rearrange("p (j w) r -> p r j w", w=2),
+            )
+
+        def quantise_y(u):
+            m = slice(CELLS * u, CELLS * (u + 1))
+            nc.vector.quantize_mx(out=y_codes[:, m].bitcast(FP8X4), scales=y_scales[:, m], in_=t["y_t", u][:])
+            dst = out_1[0].rearrange("p m t -> p (m t)").bitcast(I32)
+            nc.sync.dma_start(out=dst[:, m], in_=y_codes[:, m].bitcast(I32))
+
+        def store_scales(m):
+            for q in range(4):
+                nc.sync.dma_start(
+                    out=out_2[0, 4 * q : 4 * q + 4, m].bitcast(I32), in_=y_scales[32 * q : 32 * q + 4, m].bitcast(I32)
+                )
+
+        def front(fn, f, *rest):
+            if 0 <= f < len(FRONT):
+                fn(f, *rest)
+
+        def back(fn, f, k):
+            if 0 <= f < len(FRONT) and k < FRONT[f][2]:
+                fn(FRONT[f][0], FRONT[f][1] + k)
+
+        def whole(fn, f):
+            if 0 <= f < len(FRONT) and FRONT[f][1] + FRONT[f][2] == TILES:
+                fn(FRONT[f][0])
+
+        turn_lam(0)
+        lay_lam(0)
+        turn_lam(1)
+        permute_f(0, 0)
+        quantise_lam(0)
+        lay_lam(1)
+        mm_z(0, 0, 0)
+        permute_f(0, 1)
+        mm_z(0, 1, 0)
+        quantise_lam(1)
+        nc.vector.tensor_copy(ident_bf[:], ident[:])
+        exp_z(0, 0, 0)
+        turn_lam(2)
+        mm_z(1, 0, 0)
+        exp_z(0, 1, 0)
+        permute_codes(1, 0)
+        times_k(0, 0)
+        lay_lam(2)
+        mm_z(1, 1, 0)
+        turn_k()
+        times_k(0, 1)
+        exp_z(1, 0, 0)
+        turn_lam(3)
+        quantise_conc(0, 0)
+        quantise_lam(2)
+        quantise_conc(0, 1)
+        exp_z(1, 1, 0)
+        nc.scalar.copy(k_rows[:], t["k_bank"][:])
+        lay_lam(3)
+        mm_z(2, 0, 0)
+        mm_z(2, 0, 1)
+        mm_z(2, 1, 0)
+        spread_constants()
+        permute_codes(1, 1)
+        permute_scales(1, 0)
+        permute_scales(1, 1)
+        quantise_lam(3)
+        PERM = {1: [(2, 0), (2, 1)], 2: [(3, 0)], 3: [(3, 1)]}
+        for f in range(1, len(FRONT)):
+            front(turn_lam, f + 3)
+            back(turn_y, f - 3, 0)
+            back(turn_y, f - 3, 1)
+            back(balance, f - 2, 0)
+            back(times_mass, f - 2, 0)
+            front(exp_z, f + 1, 0, 0)
+            front(mm_z, f + 1, 1, 1)
+            back(balance, f - 2, 1)
+            back(times_mass, f - 2, 1)
+            back(mm_b, f - 1, 0)
+            front(exp_z, f + 1, 0, 1)
+            front(mm_z, f + 2, 0, 0)
+            front(lay_lam, f + 3)
+            front(times_k, f, 0)
+            front(exp_z, f + 1, 1, 0)
+            front(mm_z, f + 2, 0, 1)
+            whole(lay_y, f - 3)
+            front(times_k, f, 1)
+            front(exp_z, f + 1, 1, 1)
+            front(mm_z, f + 2, 1, 0)
+            back(mm_b, f - 1, 1)
+            back(round_y, f - 2, 0)
+            back(round_y, f - 2, 1)
+            front(quantise_conc, f, 0)
+            whole(quantise_y, f - 3)
+            front(quantise_conc, f, 1)
+            front(quantise_lam, f + 3)
+            for c, g in PERM.get(f, []):
+                permute_f(c, g)
+        a, b, c = UNITS - 3, UNITS - 2, UNITS - 1
+        store_scales(slice(0, CELLS * a))
+        turn_y(a, 0)
+        turn_y(a, 1)
+        lay_y(a)
+        balance(b, 0)
+        times_mass(b, 0)
+        mm_b(c, 0)
+        balance(b, 1)
+        times_mass(b, 1)
+        mm_b(c, 1)
+        round_y(b, 0)
+        balance(c, 0)
+        balance(c, 1)
+        round_y(b, 1)
+        round_y_v(c, 0)
+        turn_y(b, 0)
+        turn_y(b, 1)
+        lay_y(b)
+        times_mass(c, 0)
+        round_y_v(c, 1)
+        turn_y(c, 0)
+        turn_y(c, 1)
+        lay_y(c)
+        times_mass_v(c, 1)
+        quantise_y(a)
+        quantise_y(b)
+        quantise_y(c)
+        store_scales(slice(CELLS * a, CELLS * UNITS))

@@ -45,8 +45,10 @@ def tile_grouped_mass_action_balance_k7_kernel(
         tot_sb = [keep.tile([P, TILES, E], BF16, name="tot%d" % u) for u in range(UNITS)]
         f_raw = [keep.tile([P, 2 * S], U8, name="fraw%d" % c) for c in range(G)]
         f_perm = [keep.tile([P, 2 * S], U8, name="fperm%d" % c, align_bytes=64) for c in range(G)]
-        fs_raw = keep.tile([P, G, S], U8)
-        fs_perm = [keep.tile([P, S], U8, name="fsperm%d" % c, align_bytes=64) for c in range(G)]
+        fs_raw = keep.tile([P, S], U8)
+        fs_first = keep.tile([P, S], U8, align_bytes=64)
+        fs_rest = keep.tile([P, G - 1, S], U8, align_bytes=64)
+        fs_perm = [fs_first] + [fs_rest[:, c, :] for c in range(G - 1)]
         h_sb = [keep.tile([P, GROUPS, 2 * E], U8, name="h%d" % c, align_bytes=64) for c in range(G)]
         hs_sb = keep.tile([P, G * GROUPS, E], U8, align_bytes=64)
         k_sb = keep.tile([P, P], BF16)
@@ -64,12 +66,13 @@ def tile_grouped_mass_action_balance_k7_kernel(
         mass4 = keep.tile([P, PACK], BF16)
 
         nc.vector.memset(warm[:], 0.0)
-        nc.vector.memset(fs_raw[:, 0, :].bitcast(I32), 0)
+        nc.vector.memset(fs_raw[:].bitcast(I32), 0)
         make_identity(nc, ident[:])
         nc.scalar.activation(warm[:], warm[:], ACT.Exp)
         nc.vector.memset(k_sb[:], 0.0)
-        nc.vector.memset(fs_raw[:, 1:G, :].rearrange("p c n -> p (c n)").bitcast(I32), 0)
-        nc.gpsimd.memset(hs_sb[:].rearrange("p c n -> p (c n)").bitcast(I32), 0)
+        nc.vector.tensor_copy(ident_bf[:], ident[:])
+        nc.vector.memset(fs_rest[:].rearrange("p c n -> p (c n)").bitcast(I32), 0)
+        nc.vector.memset(hs_sb[:].rearrange("p c n -> p (c n)").bitcast(I32), 0)
 
         def load_lam(u):
             nc.sync.dma_start(out=lam_sb[u][:], in_=rows_of(lam, u))
@@ -84,68 +87,63 @@ def tile_grouped_mass_action_balance_k7_kernel(
             src = h_words[GROUPS * c : GROUPS * (c + 1)].rearrange("g p n -> p g n")
             nc.sync.dma_start(out=h_sb[c][:].bitcast(I32), in_=src.bitcast(I32))
 
-        def load_scales(dst, src, lo, hi):
+        def load_h_scales(lo, hi):
             for q in range(4):
-                rows = src[lo:hi, 4 * q : 4 * q + 4, :].rearrange("g r n -> r g n")
-                nc.sync.dma_start(out=dst[32 * q : 32 * q + 4, lo:hi].bitcast(I32), in_=rows.bitcast(I32))
+                rows = h_scales[lo:hi, 4 * q : 4 * q + 4, :].rearrange("g r n -> r g n")
+                nc.sync.dma_start(out=hs_sb[32 * q : 32 * q + 4, lo:hi].bitcast(I32), in_=rows.bitcast(I32))
 
-        nc.sync.dma_start(out=lam_sb[0][:, 0, :], in_=rows_of(lam, 0)[:, 0, :])
-        load_f(0, 0, S)
-        load_scales(fs_raw, f_scales, 0, 1)
-        nc.sync.dma_start(out=lam_sb[0][:, 1, :], in_=rows_of(lam, 0)[:, 1, :])
-        load_f(0, S, 2 * S)
-        k_src = kform.rearrange("c (g p t) -> p (c g) t", g=GROUPS, t=PACK)
-        nc.sync.dma_start(out=k_sb[:, 0 : PACK * G * GROUPS].rearrange("p (x t) -> p x t", t=PACK), in_=k_src)
-        load_lam(1)
-        load_f(1)
-        load_lam(2)
-        load_scales(fs_raw, f_scales, 1, G)
-        nc.sync.dma_start(out=mass4[:], in_=mass.rearrange("(p t) -> p t", t=PACK))
-        load_scales(hs_sb, h_scales, 0, GROUPS)
-        load_h(0)
-        load_f(2)
-        load_lam(3)
-        load_total(0)
-        nc.sync.dma_start(out=vol_sb[:], in_=vol.rearrange("c (h p j) -> p (c h) j", p=P, j=TILES))
-        nc.sync.dma_start(out=mass_sb[:], in_=mass.partition_broadcast(P))
-        load_f(3)
-        load_lam(4)
-        load_total(1)
-        load_scales(hs_sb, h_scales, GROUPS, G * GROUPS)
-        for u in range(2, UNITS):
-            if u % PER_SYS == 0:
-                load_h(u // PER_SYS)
-            if u + 3 < UNITS:
-                load_lam(u + 3)
-            load_total(u)
-        nc.gpsimd.tensor_scalar(neg_vol[:], vol_sb[:].rearrange("p u j -> p (u j)"), -1.0, 0.0, ALU.mult, ALU.add)
+        def load_first_lam(j):
+            nc.sync.dma_start(out=lam_sb[0][:, j, :], in_=rows_of(lam, 0)[:, j, :])
+
+        def load_f_scales():
+            for q in range(4):
+                rows = f_scales[:, 4 * q : 4 * q + 4, :]
+                nc.sync.dma_start(out=fs_raw[32 * q : 32 * q + 4 * G, :].bitcast(I32), in_=rows.bitcast(I32))
+
+        def load_k():
+            k_src = kform.rearrange("c (g p t) -> p (c g) t", g=GROUPS, t=PACK)
+            nc.sync.dma_start(out=k_sb[:, 0 : PACK * G * GROUPS].rearrange("p (x t) -> p x t", t=PACK), in_=k_src)
+
+        def load_vol():
+            nc.sync.dma_start(out=vol_sb[:], in_=vol.rearrange("c (h p j) -> p (c h) j", p=P, j=TILES))
+            nc.gpsimd.tensor_scalar(neg_vol[:], vol_sb[:].rearrange("p u j -> p (u j)"), -1.0, 0.0, ALU.mult, ALU.add)
+
+        def load_mass():
+            nc.sync.dma_start(out=mass_sb[:], in_=mass.partition_broadcast(P))
+
+        def load_mass4():
+            nc.sync.dma_start(out=mass4[:], in_=mass.rearrange("(p t) -> p t", t=PACK))
+
 
         t = {}
 
         def live(u):
             return 0 <= u < UNITS
 
-        def permute_codes(c, g):
-            w = slice(2 * KP * g, 2 * KP * (g + 1))
+        def permute_codes(c, lo, hi):
+            w = slice(2 * KP * lo, 2 * KP * hi)
             nc.vector.tensor_copy(
-                f_perm[c][:, w].rearrange("p (t m b) -> p t m b", t=PACK, b=2),
-                f_raw[c][:, w].rearrange("p (m t b) -> p t m b", t=PACK, b=2),
+                f_perm[c][:, w].rearrange("p (g t m b) -> p g t m b", t=PACK, m=P, b=2),
+                f_raw[c][:, w].rearrange("p (g m t b) -> p g t m b", t=PACK, m=P, b=2),
             )
 
-        def permute_scales(c, g):
-            s = slice(KP * g, KP * (g + 1))
+        def permute_scales():
             nc.vector.tensor_copy(
-                fs_perm[c][:, s].rearrange("p (t m) -> p t m", t=PACK),
-                fs_raw[:, c, s].rearrange("p (m t) -> p t m", t=PACK),
+                fs_first[:].rearrange("p (g t m) -> p g t m", t=PACK, m=P),
+                fs_raw[:].rearrange("p (g m t) -> p g t m", t=PACK, m=P),
             )
 
-        def permute_f(c, g):
-            permute_codes(c, g)
-            permute_scales(c, g)
+        def move_scales(c):
+            for q in range(4):
+                src = fs_first[32 * q + 4 * c : 32 * q + 4 * c + 4, :]
+                nc.sync.dma_start(out=fs_perm[c][32 * q : 32 * q + 4, :].bitcast(I32), in_=src.bitcast(I32))
 
         def turn_lam(f):
             u, j0, n = FRONT[f]
-            bank = psum.tile([P, n * 2, P], F32, tag=("turn_y" if f == 1 else "turn_lam"), name="lam_bank")
+            if f in (2, 3):
+                bank = psum.tile([P, n * 2, P], F32, tag="b", name="lam_bank", bufs=2)
+            else:
+                bank = psum.tile([P, n * 2, P], F32, tag=("turn_y" if f == 1 else "turn_lam"), name="lam_bank")
             t["lam_bank", f] = bank
             for j in range(n):
                 words = lam_sb[u][:, j0 + j, :].bitcast(F32)
@@ -154,7 +152,7 @@ def tile_grouped_mass_action_balance_k7_kernel(
 
         def lay_lam(f):
             n = FRONT[f][2]
-            lam_t = work.tile([P, n * KP], BF16, tag="lam_t", name="lam_t", align_bytes=64)
+            lam_t = work.tile([P, n * KP], BF16, tag="lam_t", name="lam_t", bufs=3, align_bytes=64)
             t["lam_t", f] = lam_t
             nc.scalar.copy(
                 lam_t[:].bitcast(F32).rearrange("p (j r w) -> p j r w", j=n, w=2),
@@ -163,8 +161,8 @@ def tile_grouped_mass_action_balance_k7_kernel(
 
         def quantise_lam(f):
             n = FRONT[f][2]
-            codes = work.tile([P, n * P], U32, tag="lam_codes", name="lam_codes", bufs=3, align_bytes=64)
-            scales = work.tile([P, n * P], U8, tag="lam_scales", name="lam_scales", bufs=3, align_bytes=64)
+            codes = work.tile([P, n * P], U32, tag="lam_codes", name="lam_codes", bufs=4, align_bytes=64)
+            scales = work.tile([P, n * P], U8, tag="lam_scales", name="lam_scales", bufs=4, align_bytes=64)
             t["lam_q", f] = (codes, scales)
             nc.vector.quantize_mx(out=codes[:].bitcast(FP8X4), scales=scales[:], in_=t["lam_t", f][:])
 
@@ -199,28 +197,34 @@ def tile_grouped_mass_action_balance_k7_kernel(
 
         def times_k(f, g):
             u, j0, n = FRONT[f]
-            conc = work.tile([P, n * KP], BF16, tag="conc", name="conc", bufs=3, align_bytes=64)
-            t["conc", f, g] = conc
+            if g == 0:
+                t["conc", f] = work.tile([P, GROUPS, n * KP], BF16, tag="conc", name="conc", align_bytes=64)
             k0 = PACK * (GROUPS * (u // PER_SYS) + g)
             k_view = (k_sb if f < 2 else k_ps)[:, k0 : k0 + PACK].rearrange("p (a e) -> p a e", a=n).unsqueeze(1)
             nc.vector.tensor_tensor(
-                conc[:].rearrange("p (n a e) -> p n a e", a=n, e=PACK // n),
+                t["conc", f][:, g, :].rearrange("p (n a e) -> p n a e", a=n, e=PACK // n),
                 t["ex", f, g][:].rearrange("p a n e -> p n a e"),
                 k_view.to_broadcast([P, n * P, n, PACK // n]),
                 ALU.mult,
             )
 
-        def quantise_conc(f, g):
+        def quantise_conc(f):
             u, j0, n = FRONT[f]
-            codes = work.tile([P, n * P], U32, tag="conc_codes", name="conc_codes", bufs=6, align_bytes=64)
-            scales = work.tile([P, n * P], U8, tag="conc_scales", name="conc_scales", bufs=6, align_bytes=64)
-            for j in range(n):
-                t["conc_q", u, j0 + j, g] = (codes[:, P * j : P * (j + 1)], scales[:, P * j : P * (j + 1)])
-            nc.vector.quantize_mx(out=codes[:].bitcast(FP8X4), scales=scales[:], in_=t["conc", f, g][:])
+            codes = work.tile([P, GROUPS * n * P], U32, tag="conc_codes", name="conc_codes", bufs=3, align_bytes=64)
+            scales = work.tile([P, GROUPS * n * P], U8, tag="conc_scales", name="conc_scales", bufs=3, align_bytes=64)
+            for g in range(GROUPS):
+                for j in range(n):
+                    cols = slice(P * (n * g + j), P * (n * g + j + 1))
+                    t["conc_q", u, j0 + j, g] = (codes[:, cols], scales[:, cols])
+            src = t["conc", f][:].rearrange("p g x -> p (g x)")
+            nc.vector.quantize_mx(out=codes[:].bitcast(FP8X4), scales=scales[:], in_=src)
 
         def mm_b(u, j):
             c = u // PER_SYS
-            bank = psum.tile([P, E], F32, tag="b", name="b_bank", bufs=2)
+            if u == UNITS - 1:
+                bank = psum.tile([P, E], F32, tag="z", name="z_bank", bufs=3)
+            else:
+                bank = psum.tile([P, E], F32, tag="b", name="b_bank", bufs=2)
             t["b", u, j] = bank
             for g in range(GROUPS):
                 codes, scales = t["conc_q", u, j, g]
@@ -293,7 +297,7 @@ def tile_grouped_mass_action_balance_k7_kernel(
                 nc.tensor.transpose(t["y_bank", u][:, 2 * j + w, :], words[:, P * w : P * (w + 1)], ident[:])
 
         def lay_y(u):
-            y_t = work.tile([P, CELLS * PACK], BF16, tag="y_t", name="y_t", align_bytes=64)
+            y_t = work.tile([P, CELLS * PACK], BF16, tag="y_t", name="y_t", bufs=3, align_bytes=64)
             t["y_t", u] = y_t
             nc.scalar.copy(
                 y_t[:].bitcast(F32).rearrange("p (r j w) -> p r j w", j=TILES, w=2),
@@ -306,9 +310,9 @@ def tile_grouped_mass_action_balance_k7_kernel(
             dst = out_1[0].rearrange("p m t -> p (m t)").bitcast(I32)
             nc.sync.dma_start(out=dst[:, m], in_=y_codes[:, m].bitcast(I32))
 
-        def store_scales(m):
+        def store_scales(m, queue):
             for q in range(4):
-                nc.sync.dma_start(
+                queue.dma_start(
                     out=out_2[0, 4 * q : 4 * q + 4, m].bitcast(I32), in_=y_scales[32 * q : 32 * q + 4, m].bitcast(I32)
                 )
 
@@ -324,44 +328,77 @@ def tile_grouped_mass_action_balance_k7_kernel(
             if 0 <= f < len(FRONT) and FRONT[f][1] + FRONT[f][2] == TILES:
                 fn(FRONT[f][0])
 
+        load_first_lam(0)
+        load_f(0, 0, S)
+        load_f_scales()
+        load_first_lam(1)
+        load_lam(1)
+        load_f(0, S, 2 * S)
+        load_f(1)
+        load_k()
+        load_f(2)
+        load_lam(2)
         turn_lam(0)
         lay_lam(0)
         turn_lam(1)
-        permute_f(0, 0)
+        permute_codes(0, 0, 1)
+        permute_scales()
+        move_scales(1)
+        load_mass4()
+        load_h_scales(0, GROUPS)
+        load_h(0)
+        load_lam(3)
+        load_total(0)
+        load_vol()
+        load_mass()
+        load_f(3)
+        load_lam(4)
+        load_total(1)
+        load_h_scales(GROUPS, G * GROUPS)
+        move_scales(2)
+        move_scales(3)
+        load_h(1)
+        load_lam(5)
+        load_total(2)
+        load_lam(6)
+        load_total(3)
+        load_h(2)
+        load_lam(7)
+        load_total(4)
+        load_total(5)
+        load_h(3)
+        load_total(6)
+        load_total(7)
         quantise_lam(0)
         lay_lam(1)
+        turn_lam(2)
         mm_z(0, 0, 0)
-        permute_f(0, 1)
+        permute_codes(0, 1, 2)
         mm_z(0, 1, 0)
         quantise_lam(1)
-        nc.vector.tensor_copy(ident_bf[:], ident[:])
+        lay_lam(2)
         exp_z(0, 0, 0)
-        turn_lam(2)
         mm_z(1, 0, 0)
         exp_z(0, 1, 0)
-        permute_codes(1, 0)
-        times_k(0, 0)
-        lay_lam(2)
         mm_z(1, 1, 0)
-        turn_k()
-        times_k(0, 1)
-        exp_z(1, 0, 0)
-        turn_lam(3)
-        quantise_conc(0, 0)
+        permute_codes(1, 0, 2)
         quantise_lam(2)
-        quantise_conc(0, 1)
-        exp_z(1, 1, 0)
-        nc.scalar.copy(k_rows[:], t["k_bank"][:])
-        lay_lam(3)
+        permute_codes(2, 0, 1)
+        times_k(0, 0)
+        exp_z(1, 0, 0)
         mm_z(2, 0, 0)
+        turn_lam(3)
+        times_k(0, 1)
+        permute_codes(2, 1, 2)
+        quantise_conc(0)
+        exp_z(1, 1, 0)
         mm_z(2, 0, 1)
+        lay_lam(3)
         mm_z(2, 1, 0)
-        spread_constants()
-        permute_codes(1, 1)
-        permute_scales(1, 0)
-        permute_scales(1, 1)
+        turn_k()
         quantise_lam(3)
-        PERM = {1: [(2, 0), (2, 1)], 2: [(3, 0)], 3: [(3, 1)]}
+        nc.scalar.copy(k_rows[:], t["k_bank"][:])
+        PERM = {1: 3}
         for f in range(1, len(FRONT)):
             front(turn_lam, f + 3)
             back(turn_y, f - 3, 0)
@@ -384,40 +421,41 @@ def tile_grouped_mass_action_balance_k7_kernel(
             front(exp_z, f + 1, 1, 1)
             front(mm_z, f + 2, 1, 0)
             back(mm_b, f - 1, 1)
+            if f == 1:
+                spread_constants()
             back(round_y, f - 2, 0)
             back(round_y, f - 2, 1)
-            front(quantise_conc, f, 0)
+            if f in PERM:
+                permute_codes(PERM[f], 0, GROUPS)
             whole(quantise_y, f - 3)
-            front(quantise_conc, f, 1)
             front(quantise_lam, f + 3)
-            for c, g in PERM.get(f, []):
-                permute_f(c, g)
+            front(quantise_conc, f)
         a, b, c = UNITS - 3, UNITS - 2, UNITS - 1
-        store_scales(slice(0, CELLS * a))
+        store_scales(slice(0, CELLS * a), nc.sync)
+        mm_b(c, 0)
+        mm_b(c, 1)
         turn_y(a, 0)
         turn_y(a, 1)
         lay_y(a)
         balance(b, 0)
         times_mass(b, 0)
-        mm_b(c, 0)
         balance(b, 1)
         times_mass(b, 1)
-        mm_b(c, 1)
         round_y(b, 0)
         balance(c, 0)
         balance(c, 1)
         round_y(b, 1)
         round_y_v(c, 0)
-        turn_y(b, 0)
-        turn_y(b, 1)
-        lay_y(b)
-        times_mass(c, 0)
         round_y_v(c, 1)
+        turn_y(b, 0)
         turn_y(c, 0)
         turn_y(c, 1)
+        turn_y(b, 1)
         lay_y(c)
+        lay_y(b)
         times_mass_v(c, 1)
+        times_mass(c, 0)
         quantise_y(a)
-        quantise_y(b)
         quantise_y(c)
-        store_scales(slice(CELLS * a, CELLS * UNITS))
+        quantise_y(b)
+        store_scales(slice(CELLS * a, CELLS * UNITS), nc.scalar)

@@ -24,6 +24,7 @@ TILES = CELLS // P
 UNITS = G * R // CELLS
 PER_SYS = R // CELLS
 GROUPS = S // KP
+VOL_ROW = PACK * G * GROUPS
 FRONT = [(0, j, 1) for j in range(TILES)] + [(u, 0, TILES) for u in range(1, UNITS)]
 
 
@@ -51,9 +52,8 @@ def tile_grouped_mass_action_balance_k7_kernel(
         fs_perm = [fs_first] + [fs_rest[:, c, :] for c in range(G - 1)]
         h_sb = [keep.tile([P, GROUPS, 2 * E], U8, name="h%d" % c, align_bytes=64) for c in range(G)]
         hs_sb = keep.tile([P, G * GROUPS, E], U8, align_bytes=64)
-        k_sb = keep.tile([P, P], BF16)
-        k_rows = keep.tile([P, P], BF16)
-        vol_sb = keep.tile([P, UNITS, TILES], BF16)
+        rows_sb = keep.tile([P, KP], BF16)
+        vol_rows = keep.tile([P, CELLS], BF16)
         neg_vol = keep.tile([P, UNITS * TILES], F32)
         mass_sb = keep.tile([P, E], BF16)
         ident = keep.tile([P, P], F32)
@@ -69,7 +69,8 @@ def tile_grouped_mass_action_balance_k7_kernel(
         nc.vector.memset(fs_raw[:].bitcast(I32), 0)
         make_identity(nc, ident[:])
         nc.scalar.activation(warm[:], warm[:], ACT.Exp)
-        nc.vector.memset(k_sb[:], 0.0)
+        nc.vector.memset(rows_sb[:], 0.0)
+        nc.vector.memset(vol_rows[:], 0.0)
         nc.vector.tensor_copy(ident_bf[:], ident[:])
         nc.vector.memset(fs_rest[:].rearrange("p c n -> p (c n)").bitcast(I32), 0)
         nc.vector.memset(hs_sb[:].rearrange("p c n -> p (c n)").bitcast(I32), 0)
@@ -101,15 +102,17 @@ def tile_grouped_mass_action_balance_k7_kernel(
                 nc.sync.dma_start(out=fs_raw[32 * q : 32 * q + 4 * G, :].bitcast(I32), in_=rows.bitcast(I32))
 
         def load_k():
-            k_src = kform.rearrange("c (g p t) -> p (c g) t", g=GROUPS, t=PACK)
-            nc.sync.dma_start(out=k_sb[:, 0 : PACK * G * GROUPS].rearrange("p (x t) -> p x t", t=PACK), in_=k_src)
+            k_flat = kform.rearrange("c (g x) -> (c g) x", g=GROUPS)
+            span = KP - PACK + 1
+            for e in range(PACK):
+                nc.sync.dma_start(out=rows_sb[e:VOL_ROW:PACK, 0:span], in_=k_flat[:, e : e + span])
 
         def load_vol():
-            nc.sync.dma_start(out=vol_sb[:], in_=vol.rearrange("c (h p j) -> p (c h) j", p=P, j=TILES))
-            nc.gpsimd.tensor_scalar(neg_vol[:], vol_sb[:].rearrange("p u j -> p (u j)"), -1.0, 0.0, ALU.mult, ALU.add)
-
-        def load_mass():
-            nc.sync.dma_start(out=mass_sb[:], in_=mass.partition_broadcast(P))
+            vol_flat = vol.rearrange("c (h x) -> (c h) x", x=CELLS)
+            span = CELLS - TILES + 1
+            for j in range(TILES):
+                dst = vol_rows[j : UNITS * TILES : TILES, 0:span]
+                nc.sync.dma_start(out=dst, in_=vol_flat[:, j : j + span])
 
         def load_mass4():
             nc.sync.dma_start(out=mass4[:], in_=mass.rearrange("(p t) -> p t", t=PACK))
@@ -200,7 +203,7 @@ def tile_grouped_mass_action_balance_k7_kernel(
             if g == 0:
                 t["conc", f] = work.tile([P, GROUPS, n * KP], BF16, tag="conc", name="conc", align_bytes=64)
             k0 = PACK * (GROUPS * (u // PER_SYS) + g)
-            k_view = (k_sb if f < 2 else k_ps)[:, k0 : k0 + PACK].rearrange("p (a e) -> p a e", a=n).unsqueeze(1)
+            k_view = k_ps[:, k0 : k0 + PACK].rearrange("p (a e) -> p a e", a=n).unsqueeze(1)
             nc.vector.tensor_tensor(
                 t["conc", f][:, g, :].rearrange("p (n a e) -> p n a e", a=n, e=PACK // n),
                 t["ex", f, g][:].rearrange("p a n e -> p n a e"),
@@ -239,14 +242,24 @@ def tile_grouped_mass_action_balance_k7_kernel(
                 )
 
         def turn_k():
-            bank = psum.tile([P, P], BF16, tag="turn_y", name="k_bank")
-            nc.tensor.transpose(bank[:], k_sb[:], ident_bf[:])
-            t["k_bank"] = bank
+            nc.tensor.transpose(k_ps, rows_sb[:, 0:KP:PACK], ident_bf[:])
 
-        def spread_constants():
-            nc.tensor.transpose(k_ps, k_rows[:], ident_bf[:])
+        def spread_mass():
             for e in range(PACK):
                 nc.tensor.transpose(consts[:, e, :], mass4[:, e : e + 1].to_broadcast([P, P]), ident_bf[:])
+
+        def turn_vol():
+            bank = psum.tile([P, P], BF16, tag="turn_y", name="vol_bank")
+            t["vol_bank"] = bank
+            nc.tensor.transpose(bank[:], vol_rows[:, 0:CELLS:TILES], ident_bf[:])
+
+        def negate_vol():
+            nc.vector.tensor_scalar(neg_vol[:], t["vol_bank"][:, 0 : UNITS * TILES], -1.0, None, ALU.mult)
+
+        def copy_mass():
+            nc.vector.tensor_copy(
+                mass_sb[:].rearrange("r (q e) -> r q e", e=PACK), consts[:, 0:PACK, :].rearrange("r e q -> r q e")
+            )
 
         def balance(u, j):
             res = work.tile([P, E], F32, tag="res", name="res", bufs=4)
@@ -257,10 +270,12 @@ def tile_grouped_mass_action_balance_k7_kernel(
             )
 
         def times_mass(u, j):
-            y = work.tile([P, E], F32, tag="y", name="y", bufs=6)
+            if j == 0:
+                t["y2", u] = work.tile([P, TILES, E], F32, tag="y2", name="y2", bufs=3)
+            y = t["y2", u][:, j, :]
             t["y", u, j] = y
-            nc.gpsimd.tensor_tensor(y[:], t["res", u, j][:], mass_sb[:], ALU.mult)
-            nc.sync.dma_start(out=rows_of(out_0, u)[:, j, :], in_=y[:])
+            nc.gpsimd.tensor_tensor(y, t["res", u, j][:], mass_sb[:], ALU.mult)
+            nc.sync.dma_start(out=rows_of(out_0, u)[:, j, :], in_=y)
 
         def times_mass_v(u, j):
             y = work.tile([P, E], F32, tag="y", name="y", bufs=6)
@@ -275,13 +290,20 @@ def tile_grouped_mass_action_balance_k7_kernel(
 
         def round_y(u, j):
             y_bf = work.tile([P, E], BF16, tag="y_bf", name="y_bf", bufs=4)
-            t["y_bf", u, j] = y_bf
+            t["y_bf", u, j] = y_bf[:]
             dst = y_bf[:].rearrange("r (w q e) -> r w q e", w=2, e=2)
-            nc.scalar.copy(dst, t["y", u, j][:].rearrange("r (q w e) -> r w q e", w=2, e=2))
+            nc.scalar.copy(dst, t["y", u, j].rearrange("r (q w e) -> r w q e", w=2, e=2))
+
+        def round_pair(u):
+            y_bf = work.tile([P, TILES, E], BF16, tag="y_bf2", name="y_bf2", bufs=2)
+            for j in range(TILES):
+                t["y_bf", u, j] = y_bf[:, j, :]
+            dst = y_bf[:].rearrange("r j (w q e) -> r j w q e", w=2, e=2)
+            nc.scalar.copy(dst, t["y2", u][:].rearrange("r j (q w e) -> r j w q e", w=2, e=2))
 
         def round_y_v(u, j):
             y_bf = work.tile([P, E], BF16, tag="y_bf", name="y_bf", bufs=4)
-            t["y_bf", u, j] = y_bf
+            t["y_bf", u, j] = y_bf[:]
             nc.vector.tensor_tensor(
                 y_bf[:].rearrange("r (w q e) -> r w q e", w=2, e=2),
                 t["res", u, j][:].rearrange("r (q w e) -> r w q e", w=2, e=2),
@@ -292,9 +314,13 @@ def tile_grouped_mass_action_balance_k7_kernel(
         def turn_y(u, j):
             if j == 0:
                 t["y_bank", u] = psum.tile([P, TILES * 2, P], F32, tag=("turn_lam" if u == UNITS - 1 else "turn_y"), name="y_bank")
-            words = t["y_bf", u, j][:].bitcast(F32)
+            words = t["y_bf", u, j].bitcast(F32)
             for w in range(2):
                 nc.tensor.transpose(t["y_bank", u][:, 2 * j + w, :], words[:, P * w : P * (w + 1)], ident[:])
+
+        def turn_pair(u):
+            for j in range(TILES):
+                turn_y(u, j)
 
         def lay_y(u):
             y_t = work.tile([P, CELLS * PACK], BF16, tag="y_t", name="y_t", bufs=3, align_bytes=64)
@@ -334,36 +360,35 @@ def tile_grouped_mass_action_balance_k7_kernel(
         load_first_lam(1)
         load_lam(1)
         load_f(0, S, 2 * S)
-        load_f(1)
         load_k()
+        load_f(1)
         load_f(2)
         load_lam(2)
+        load_mass4()
+        load_vol()
+        load_lam(3)
+        load_h_scales(0, GROUPS)
+        load_h(0)
+        load_f(3)
         turn_lam(0)
         lay_lam(0)
         turn_lam(1)
         permute_codes(0, 0, 1)
         permute_scales()
         move_scales(1)
-        load_mass4()
-        load_h_scales(0, GROUPS)
-        load_h(0)
-        load_lam(3)
         load_total(0)
-        load_vol()
-        load_mass()
-        load_f(3)
         load_lam(4)
         load_total(1)
         load_h_scales(GROUPS, G * GROUPS)
-        move_scales(2)
-        move_scales(3)
         load_h(1)
         load_lam(5)
+        move_scales(2)
         load_total(2)
         load_lam(6)
         load_total(3)
         load_h(2)
         load_lam(7)
+        move_scales(3)
         load_total(4)
         load_total(5)
         load_h(3)
@@ -372,6 +397,7 @@ def tile_grouped_mass_action_balance_k7_kernel(
         quantise_lam(0)
         lay_lam(1)
         turn_lam(2)
+        turn_k()
         mm_z(0, 0, 0)
         permute_codes(0, 1, 2)
         mm_z(0, 1, 0)
@@ -395,14 +421,13 @@ def tile_grouped_mass_action_balance_k7_kernel(
         mm_z(2, 0, 1)
         lay_lam(3)
         mm_z(2, 1, 0)
-        turn_k()
+        spread_mass()
+        turn_vol()
         quantise_lam(3)
-        nc.scalar.copy(k_rows[:], t["k_bank"][:])
         PERM = {1: 3}
         for f in range(1, len(FRONT)):
             front(turn_lam, f + 3)
-            back(turn_y, f - 3, 0)
-            back(turn_y, f - 3, 1)
+            whole(turn_pair, f - 3)
             back(balance, f - 2, 0)
             back(times_mass, f - 2, 0)
             front(exp_z, f + 1, 0, 0)
@@ -422,9 +447,9 @@ def tile_grouped_mass_action_balance_k7_kernel(
             front(mm_z, f + 2, 1, 0)
             back(mm_b, f - 1, 1)
             if f == 1:
-                spread_constants()
-            back(round_y, f - 2, 0)
-            back(round_y, f - 2, 1)
+                negate_vol()
+                copy_mass()
+            whole(round_pair, f - 2)
             if f in PERM:
                 permute_codes(PERM[f], 0, GROUPS)
             whole(quantise_y, f - 3)

@@ -211,28 +211,28 @@ def tile_grouped_mass_action_balance_k7_kernel(
                 ALU.mult,
             )
 
-        def quantise_conc(f):
+        def quantise_conc(f, lo=0, hi=GROUPS):
             u, j0, n = FRONT[f]
-            codes = work.tile([P, GROUPS * n * P], U32, tag="conc_codes", name="conc_codes", bufs=3, align_bytes=64)
-            scales = work.tile([P, GROUPS * n * P], U8, tag="conc_scales", name="conc_scales", bufs=3, align_bytes=64)
-            for g in range(GROUPS):
+            width = (hi - lo) * n * P
+            codes = work.tile([P, width], U32, tag="conc_codes", name="conc_codes", bufs=4, align_bytes=64)
+            scales = work.tile([P, width], U8, tag="conc_scales", name="conc_scales", bufs=4, align_bytes=64)
+            for g in range(lo, hi):
                 for j in range(n):
-                    cols = slice(P * (n * g + j), P * (n * g + j + 1))
+                    cols = slice(P * (n * (g - lo) + j), P * (n * (g - lo) + j + 1))
                     t["conc_q", u, j0 + j, g] = (codes[:, cols], scales[:, cols])
-            src = t["conc", f][:].rearrange("p g x -> p (g x)")
+            src = t["conc", f][:, lo:hi, :].rearrange("p g x -> p (g x)")
             nc.vector.quantize_mx(out=codes[:].bitcast(FP8X4), scales=scales[:], in_=src)
 
-        def mm_b(u, j):
+        def mm_b(u, j, lo=0, hi=GROUPS):
             c = u // PER_SYS
-            if u == UNITS - 1:
-                bank = psum.tile([P, E], F32, tag="z", name="z_bank", bufs=3)
-            else:
-                bank = psum.tile([P, E], F32, tag="b", name="b_bank", bufs=2)
-            t["b", u, j] = bank
-            for g in range(GROUPS):
+            if lo == 0 and u == UNITS - 1:
+                t["b", u, j] = psum.tile([P, E], F32, tag="z", name="z_bank", bufs=3)
+            elif lo == 0:
+                t["b", u, j] = psum.tile([P, E], F32, tag="b", name="b_bank", bufs=2)
+            for g in range(lo, hi):
                 codes, scales = t["conc_q", u, j, g]
                 nc.tensor.matmul_mx(
-                    out=bank[:],
+                    out=t["b", u, j][:],
                     lhsT=codes.bitcast(FP8X4),
                     lhsT_scale=scales,
                     rhs=h_sb[c][:, g, :].bitcast(FP4X4),
@@ -323,7 +323,7 @@ def tile_grouped_mass_action_balance_k7_kernel(
                 turn_y(u, j)
 
         def lay_y(u):
-            y_t = work.tile([P, CELLS * PACK], BF16, tag="y_t", name="y_t", bufs=3, align_bytes=64)
+            y_t = work.tile([P, CELLS * PACK], BF16, tag="y_t", name="y_t", bufs=4, align_bytes=64)
             t["y_t", u] = y_t
             nc.scalar.copy(
                 y_t[:].bitcast(F32).rearrange("p (r j w) -> p r j w", j=TILES, w=2),
@@ -425,11 +425,9 @@ def tile_grouped_mass_action_balance_k7_kernel(
         turn_vol()
         quantise_lam(3)
         PERM = {1: 3}
-        for f in range(1, len(FRONT)):
+        for f in range(1, len(FRONT) - 1):
             front(turn_lam, f + 3)
             whole(turn_pair, f - 3)
-            back(balance, f - 2, 0)
-            back(times_mass, f - 2, 0)
             front(exp_z, f + 1, 0, 0)
             front(mm_z, f + 1, 1, 1)
             back(balance, f - 2, 1)
@@ -454,33 +452,47 @@ def tile_grouped_mass_action_balance_k7_kernel(
                 permute_codes(PERM[f], 0, GROUPS)
             whole(quantise_y, f - 3)
             front(quantise_lam, f + 3)
+            back(balance, f - 1, 0)
             front(quantise_conc, f)
-        a, b, c = UNITS - 3, UNITS - 2, UNITS - 1
-        store_scales(slice(0, CELLS * a), nc.sync)
-        mm_b(c, 0)
-        mm_b(c, 1)
-        turn_y(a, 0)
-        turn_y(a, 1)
-        lay_y(a)
-        balance(b, 0)
-        times_mass(b, 0)
-        balance(b, 1)
-        times_mass(b, 1)
-        round_y(b, 0)
-        balance(c, 0)
-        balance(c, 1)
-        round_y(b, 1)
-        round_y_v(c, 0)
-        round_y_v(c, 1)
-        turn_y(b, 0)
-        turn_y(c, 0)
-        turn_y(c, 1)
-        turn_y(b, 1)
-        lay_y(c)
-        lay_y(b)
-        times_mass_v(c, 1)
-        times_mass(c, 0)
-        quantise_y(a)
-        quantise_y(c)
-        quantise_y(b)
-        store_scales(slice(CELLS * a, CELLS * UNITS), nc.scalar)
+            back(times_mass, f - 1, 0)
+        store_scales(slice(0, CELLS * 4), nc.sync)
+        mm_b(6, 0)
+        turn_pair(4)
+        times_k(8, 0)
+        balance(5, 1)
+        quantise_conc(8, 0, 1)
+        times_mass(5, 1)
+        mm_b(7, 0, 0, 1)
+        mm_b(6, 1)
+        lay_y(4)
+        mm_b(7, 1, 0, 1)
+        times_k(8, 1)
+        round_pair(5)
+        balance(6, 0)
+        quantise_conc(8, 1, 2)
+        quantise_y(4)
+        times_mass(6, 0)
+        mm_b(7, 0, 1, 2)
+        mm_b(7, 1, 1, 2)
+        turn_pair(5)
+        lay_y(5)
+        balance(6, 1)
+        times_mass(6, 1)
+        round_y(6, 0)
+        balance(7, 0)
+        balance(7, 1)
+        round_y(6, 1)
+        round_y_v(7, 0)
+        turn_y(6, 0)
+        round_y_v(7, 1)
+        turn_y(7, 0)
+        turn_y(7, 1)
+        turn_y(6, 1)
+        lay_y(7)
+        times_mass(7, 0)
+        times_mass_v(7, 1)
+        quantise_y(5)
+        lay_y(6)
+        quantise_y(7)
+        quantise_y(6)
+        store_scales(slice(CELLS * 4, CELLS * UNITS), nc.scalar)

from contextlib import ExitStack

import concourse.mybir as mybir
from concourse.masks import make_identity

G, R, E, S = 4, 512, 512, 1024
FLOPS = 2 * 2 * G * R * E * S

F32 = mybir.dt.float32
BF16 = mybir.dt.bfloat16
I32 = mybir.dt.int32
U32 = mybir.dt.uint32
U8 = mybir.dt.uint8
FP8X4 = mybir.dt.float8_e4m3fn_x4
FP4X4 = mybir.dt.float4_e2m1fn_x4
ACT = mybir.ActivationFunctionType
ALU = mybir.AluOpType

P = 128
PACK = 4
KP = P * PACK
CELLS = 256
TILES = CELLS // P
UNITS = G * R // CELLS
PER_SYS = R // CELLS
GROUPS = S // KP
VOL_ROW = PACK * G * GROUPS
FRONT = [(0, j, 1) for j in range(TILES)] + [(u, 0, TILES) for u in range(1, UNITS)]


def tile_grouped_mass_action_balance_k7_kernel(
    tc, lam, f_words, f_scales, kform, h_words, h_scales, vol, total, mass, out_0, out_1, out_2
):
    nc = tc.nc
    with ExitStack() as ctx:
        keep = ctx.enter_context(tc.tile_pool(name="keep", bufs=1))
        work = ctx.enter_context(tc.tile_pool(name="work", bufs=2))
        psum = ctx.enter_context(tc.psum_pool(name="psum", bufs=1))
        ctx.enter_context(tc.manual_schedule())

        def rows_of(x, u):
            c, h = divmod(u, PER_SYS)
            return x[c, h * CELLS : (h + 1) * CELLS, :].rearrange("(p j) i -> p j i", j=TILES)

        lam_sb = [keep.tile([P, TILES, E], BF16, name="lam%d" % u) for u in range(UNITS)]
        tot_sb = [keep.tile([P, TILES, E], BF16, name="tot%d" % u) for u in range(UNITS)]
        f_raw = [keep.tile([P, 2 * S], U8, name="fraw%d" % c) for c in range(G)]
        f_perm = [keep.tile([P, 2 * S], U8, name="fperm%d" % c, align_bytes=64) for c in range(G)]
        fs_raw = keep.tile([P, S], U8)
        fs_first = keep.tile([P, S], U8, align_bytes=64)
        fs_rest = keep.tile([P, G - 1, S], U8, align_bytes=64)
        fs_perm = [fs_first] + [fs_rest[:, c, :] for c in range(G - 1)]
        h_sb = [keep.tile([P, GROUPS, 2 * E], U8, name="h%d" % c, align_bytes=64) for c in range(G)]
        hs_sb = keep.tile([P, G * GROUPS, E], U8, align_bytes=64)
        rows_sb = keep.tile([P, KP], BF16)
        vol_rows = keep.tile([P, CELLS], BF16)
        neg_vol = keep.tile([P, UNITS * TILES], F32)
        mass_sb = keep.tile([P, E], BF16)
        ident = keep.tile([P, P], F32)
        ident_bf = keep.tile([P, P], BF16)
        warm = keep.tile([P, 1], F32)
        y_codes = keep.tile([P, G * R], U32, align_bytes=64)
        y_scales = keep.tile([P, G * R], U8, align_bytes=64)
        consts = psum.tile([P, PACK + 1, P], BF16, tag="consts")
        k_ps = consts[:, PACK, :]
        mass4 = keep.tile([P, PACK], BF16)

        nc.vector.memset(warm[:], 0.0)
        nc.vector.memset(fs_raw[:].bitcast(I32), 0)
        make_identity(nc, ident[:])
        nc.scalar.activation(warm[:], warm[:], ACT.Exp)
        nc.vector.memset(rows_sb[:], 0.0)
        nc.vector.memset(vol_rows[:], 0.0)
        nc.vector.tensor_copy(ident_bf[:], ident[:])
        nc.vector.memset(fs_rest[:].rearrange("p c n -> p (c n)").bitcast(I32), 0)
        nc.vector.memset(hs_sb[:].rearrange("p c n -> p (c n)").bitcast(I32), 0)

        def load_lam(u):
            nc.sync.dma_start(out=lam_sb[u][:], in_=rows_of(lam, u))

        def load_total(u):
            nc.sync.dma_start(out=tot_sb[u][:], in_=rows_of(total, u))

        def load_f(c, lo=0, hi=2 * S):
            nc.sync.dma_start(out=f_raw[c][:, lo:hi].bitcast(I32), in_=f_words[c][:, lo:hi].bitcast(I32))

        def load_h(c):
            src = h_words[GROUPS * c : GROUPS * (c + 1)].rearrange("g p n -> p g n")
            nc.sync.dma_start(out=h_sb[c][:].bitcast(I32), in_=src.bitcast(I32))

        def load_h_scales(lo, hi):
            for q in range(4):
                rows = h_scales[lo:hi, 4 * q : 4 * q + 4, :].rearrange("g r n -> r g n")
                nc.sync.dma_start(out=hs_sb[32 * q : 32 * q + 4, lo:hi].bitcast(I32), in_=rows.bitcast(I32))

        def load_first_lam(j):
            nc.sync.dma_start(out=lam_sb[0][:, j, :], in_=rows_of(lam, 0)[:, j, :])

        def load_f_scales():
            for q in range(4):
                rows = f_scales[:, 4 * q : 4 * q + 4, :]
                nc.sync.dma_start(out=fs_raw[32 * q : 32 * q + 4 * G, :].bitcast(I32), in_=rows.bitcast(I32))

        def load_k():
            k_flat = kform.rearrange("c (g x) -> (c g) x", g=GROUPS)
            span = KP - PACK + 1
            for e in range(PACK):
                nc.sync.dma_start(out=rows_sb[e:VOL_ROW:PACK, 0:span], in_=k_flat[:, e : e + span])

        def load_vol():
            vol_flat = vol.rearrange("c (h x) -> (c h) x", x=CELLS)
            span = CELLS - TILES + 1
            for j in range(TILES):
                dst = vol_rows[j : UNITS * TILES : TILES, 0:span]
                nc.sync.dma_start(out=dst, in_=vol_flat[:, j : j + span])

        def load_mass4():
            nc.sync.dma_start(out=mass4[:], in_=mass.rearrange("(p t) -> p t", t=PACK))


        t = {}

        def live(u):
            return 0 <= u < UNITS

        def permute_codes(c, lo, hi):
            w = slice(2 * KP * lo, 2 * KP * hi)
            nc.vector.tensor_copy(
                f_perm[c][:, w].rearrange("p (g t m b) -> p g t m b", t=PACK, m=P, b=2),
                f_raw[c][:, w].rearrange("p (g m t b) -> p g t m b", t=PACK, m=P, b=2),
            )

        def permute_scales():
            nc.vector.tensor_copy(
                fs_first[:].rearrange("p (g t m) -> p g t m", t=PACK, m=P),
                fs_raw[:].rearrange("p (g m t) -> p g t m", t=PACK, m=P),
            )

        def move_scales(c):
            for q in range(4):
                src = fs_first[32 * q + 4 * c : 32 * q + 4 * c + 4, :]
                nc.sync.dma_start(out=fs_perm[c][32 * q : 32 * q + 4, :].bitcast(I32), in_=src.bitcast(I32))

        def turn_lam(f):
            u, j0, n = FRONT[f]
            if f in (2, 3):
                bank = psum.tile([P, n * 2, P], F32, tag="b", name="lam_bank", bufs=2)
            else:
                bank = psum.tile([P, n * 2, P], F32, tag=("turn_y" if f == 1 else "turn_lam"), name="lam_bank")
            t["lam_bank", f] = bank
            for j in range(n):
                words = lam_sb[u][:, j0 + j, :].bitcast(F32)
                for w in range(2):
                    nc.tensor.transpose(bank[:, 2 * j + w, :], words[:, w : E // 2 : 2], ident[:])

        def lay_lam(f):
            n = FRONT[f][2]
            lam_t = work.tile([P, n * KP], BF16, tag="lam_t", name="lam_t", bufs=3, align_bytes=64)
            t["lam_t", f] = lam_t
            nc.scalar.copy(
                lam_t[:].bitcast(F32).rearrange("p (j r w) -> p j r w", j=n, w=2),
                t["lam_bank", f][:].rearrange("p (j w) r -> p j r w", w=2),
            )

        def quantise_lam(f):
            n = FRONT[f][2]
            codes = work.tile([P, n * P], U32, tag="lam_codes", name="lam_codes", bufs=4, align_bytes=64)
            scales = work.tile([P, n * P], U8, tag="lam_scales", name="lam_scales", bufs=4, align_bytes=64)
            t["lam_q", f] = (codes, scales)
            nc.vector.quantize_mx(out=codes[:].bitcast(FP8X4), scales=scales[:], in_=t["lam_t", f][:])

        def mm_z(f, g, a):
            u, j0, n = FRONT[f]
            if a >= n:
                return
            c = u // PER_SYS
            side = PACK // n
            codes, scales = t["lam_q", f]
            bank = psum.tile([P, side, n * P], F32, tag="z", name="z_bank", bufs=3)
            t["z", f, g, a] = bank
            for e in range(side):
                col = KP * g + P * (side * a + e)
                nc.tensor.matmul_mx(
                    out=bank[:, e, :],
                    lhsT=f_perm[c][:, 2 * col : 2 * (col + P)].bitcast(FP4X4),
                    lhsT_scale=fs_perm[c][:, col : col + P],
                    rhs=codes[:].bitcast(FP8X4),
                    rhs_scale=scales[:],
                    start=True,
                    stop=True,
                )

        def exp_z(f, g, a):
            n = FRONT[f][2]
            if a >= n:
                return
            if a == 0:
                t["ex", f, g] = work.tile([P, n, n * P, PACK // n], F32, tag="ex", name="ex", bufs=4)
            nc.scalar.activation(t["ex", f, g][:, a], t["z", f, g, a][:].rearrange("p e n -> p n e"), ACT.Exp)

        def times_k(f, g):
            u, j0, n = FRONT[f]
            if g == 0:
                t["conc", f] = work.tile([P, GROUPS, n * KP], BF16, tag="conc", name="conc", align_bytes=64)
            k0 = PACK * (GROUPS * (u // PER_SYS) + g)
            k_view = k_ps[:, k0 : k0 + PACK].rearrange("p (a e) -> p a e", a=n).unsqueeze(1)
            nc.vector.tensor_tensor(
                t["conc", f][:, g, :].rearrange("p (n a e) -> p n a e", a=n, e=PACK // n),
                t["ex", f, g][:].rearrange("p a n e -> p n a e"),
                k_view.to_broadcast([P, n * P, n, PACK // n]),
                ALU.mult,
            )

        def quantise_conc(f, lo=0, hi=GROUPS):
            u, j0, n = FRONT[f]
            width = (hi - lo) * n * P
            codes = work.tile([P, width], U32, tag="conc_codes", name="conc_codes", bufs=4, align_bytes=64)
            scales = work.tile([P, width], U8, tag="conc_scales", name="conc_scales", bufs=4, align_bytes=64)
            for g in range(lo, hi):
                for j in range(n):
                    cols = slice(P * (n * (g - lo) + j), P * (n * (g - lo) + j + 1))
                    t["conc_q", u, j0 + j, g] = (codes[:, cols], scales[:, cols])
            src = t["conc", f][:, lo:hi, :].rearrange("p g x -> p (g x)")
            nc.vector.quantize_mx(out=codes[:].bitcast(FP8X4), scales=scales[:], in_=src)

        def mm_b(u, j, lo=0, hi=GROUPS):
            c = u // PER_SYS
            if lo == 0 and u == UNITS - 1:
                t["b", u, j] = psum.tile([P, E], F32, tag="z", name="z_bank", bufs=3)
            elif lo == 0:
                t["b", u, j] = psum.tile([P, E], F32, tag="b", name="b_bank", bufs=2)
            for g in range(lo, hi):
                codes, scales = t["conc_q", u, j, g]
                nc.tensor.matmul_mx(
                    out=t["b", u, j][:],
                    lhsT=codes.bitcast(FP8X4),
                    lhsT_scale=scales,
                    rhs=h_sb[c][:, g, :].bitcast(FP4X4),
                    rhs_scale=hs_sb[:, GROUPS * c + g, :],
                    start=(g == 0),
                    stop=(g == GROUPS - 1),
                )

        def turn_k():
            nc.tensor.transpose(k_ps, rows_sb[:, 0:KP:PACK], ident_bf[:])

        def spread_mass():
            for e in range(PACK):
                nc.tensor.transpose(consts[:, e, :], mass4[:, e : e + 1].to_broadcast([P, P]), ident_bf[:])

        def turn_vol():
            bank = psum.tile([P, P], BF16, tag="turn_y", name="vol_bank")
            t["vol_bank"] = bank
            nc.tensor.transpose(bank[:], vol_rows[:, 0:CELLS:TILES], ident_bf[:])

        def negate_vol():
            nc.vector.tensor_scalar(neg_vol[:], t["vol_bank"][:, 0 : UNITS * TILES], -1.0, None, ALU.mult)

        def copy_mass():
            nc.vector.tensor_copy(
                mass_sb[:].rearrange("r (q e) -> r q e", e=PACK), consts[:, 0:PACK, :].rearrange("r e q -> r q e")
            )

        def balance(u, j):
            res = work.tile([P, E], F32, tag="res", name="res", bufs=4)
            t["res", u, j] = res
            col = TILES * u + j
            nc.vector.scalar_tensor_tensor(
                res[:], t["b", u, j][:], neg_vol[:, col : col + 1], tot_sb[u][:, j, :], ALU.mult, ALU.add
            )

        def times_mass(u, j):
            if j == 0:
                t["y2", u] = work.tile([P, TILES, E], F32, tag="y2", name="y2", bufs=3)
            y = t["y2", u][:, j, :]
            t["y", u, j] = y
            nc.gpsimd.tensor_tensor(y, t["res", u, j][:], mass_sb[:], ALU.mult)
            nc.sync.dma_start(out=rows_of(out_0, u)[:, j, :], in_=y)

        def times_mass_v(u, j):
            y = work.tile([P, E], F32, tag="y", name="y", bufs=6)
            t["y", u, j] = y
            nc.vector.tensor_tensor(
                y[:].rearrange("r (q e) -> r q e", e=PACK),
                t["res", u, j][:].rearrange("r (q e) -> r q e", e=PACK),
                consts[:, 0:PACK, :].rearrange("r e q -> r q e"),
                ALU.mult,
            )
            nc.sync.dma_start(out=rows_of(out_0, u)[:, j, :], in_=y[:])

        def round_y(u, j):
            y_bf = work.tile([P, E], BF16, tag="y_bf", name="y_bf", bufs=4)
            t["y_bf", u, j] = y_bf[:]
            dst = y_bf[:].rearrange("r (w q e) -> r w q e", w=2, e=2)
            nc.scalar.copy(dst, t["y", u, j].rearrange("r (q w e) -> r w q e", w=2, e=2))

        def round_pair(u):
            y_bf = work.tile([P, TILES, E], BF16, tag="y_bf2", name="y_bf2", bufs=2)
            for j in range(TILES):
                t["y_bf", u, j] = y_bf[:, j, :]
            dst = y_bf[:].rearrange("r j (w q e) -> r j w q e", w=2, e=2)
            nc.scalar.copy(dst, t["y2", u][:].rearrange("r j (q w e) -> r j w q e", w=2, e=2))

        def round_y_v(u, j):
            y_bf = work.tile([P, E], BF16, tag="y_bf", name="y_bf", bufs=4)
            t["y_bf", u, j] = y_bf[:]
            nc.vector.tensor_tensor(
                y_bf[:].rearrange("r (w q e) -> r w q e", w=2, e=2),
                t["res", u, j][:].rearrange("r (q w e) -> r w q e", w=2, e=2),
                consts[:, 0:PACK, :].rearrange("r (w e) q -> r w q e", w=2),
                ALU.mult,
            )

        def turn_y(u, j):
            if j == 0:
                t["y_bank", u] = psum.tile([P, TILES * 2, P], F32, tag=("turn_lam" if u == UNITS - 1 else "turn_y"), name="y_bank")
            words = t["y_bf", u, j].bitcast(F32)
            for w in range(2):
                nc.tensor.transpose(t["y_bank", u][:, 2 * j + w, :], words[:, P * w : P * (w + 1)], ident[:])

        def turn_pair(u):
            for j in range(TILES):
                turn_y(u, j)

        def lay_y(u):
            y_t = work.tile([P, CELLS * PACK], BF16, tag="y_t", name="y_t", bufs=4, align_bytes=64)
            t["y_t", u] = y_t
            nc.scalar.copy(
                y_t[:].bitcast(F32).rearrange("p (r j w) -> p r j w", j=TILES, w=2),
                t["y_bank", u][:].rearrange("p (j w) r -> p r j w", w=2),
            )

        def quantise_y(u):
            m = slice(CELLS * u, CELLS * (u + 1))
            nc.vector.quantize_mx(out=y_codes[:, m].bitcast(FP8X4), scales=y_scales[:, m], in_=t["y_t", u][:])
            dst = out_1[0].rearrange("p m t -> p (m t)").bitcast(I32)
            nc.sync.dma_start(out=dst[:, m], in_=y_codes[:, m].bitcast(I32))

        def store_scales(m, queue):
            for q in range(4):
                queue.dma_start(
                    out=out_2[0, 4 * q : 4 * q + 4, m].bitcast(I32), in_=y_scales[32 * q : 32 * q + 4, m].bitcast(I32)
                )

        def front(fn, f, *rest):
            if 0 <= f < len(FRONT):
                fn(f, *rest)

        def back(fn, f, k):
            if 0 <= f < len(FRONT) and k < FRONT[f][2]:
                fn(FRONT[f][0], FRONT[f][1] + k)

        def whole(fn, f):
            if 0 <= f < len(FRONT) and FRONT[f][1] + FRONT[f][2] == TILES:
                fn(FRONT[f][0])

        load_first_lam(0)
        load_f(0, 0, S)
        load_f_scales()
        load_first_lam(1)
        load_lam(1)
        load_f(0, S, 2 * S)
        load_k()
        load_f(1)
        load_f(2)
        load_lam(2)
        load_mass4()
        load_vol()
        load_lam(3)
        load_h_scales(0, GROUPS)
        load_h(0)
        load_f(3)
        turn_lam(0)
        lay_lam(0)
        turn_lam(1)
        permute_codes(0, 0, 1)
        permute_scales()
        move_scales(1)
        load_total(0)
        load_lam(4)
        load_total(1)
        load_h_scales(GROUPS, G * GROUPS)
        load_h(1)
        load_lam(5)
        move_scales(2)
        load_total(2)
        load_lam(6)
        load_total(3)
        load_h(2)
        load_lam(7)
        move_scales(3)
        load_total(4)
        load_total(5)
        load_h(3)
        load_total(6)
        load_total(7)
        quantise_lam(0)
        lay_lam(1)
        turn_lam(2)
        turn_k()
        mm_z(0, 0, 0)
        permute_codes(0, 1, 2)
        mm_z(0, 1, 0)
        quantise_lam(1)
        lay_lam(2)
        exp_z(0, 0, 0)
        mm_z(1, 0, 0)
        exp_z(0, 1, 0)
        mm_z(1, 1, 0)
        permute_codes(1, 0, 2)
        quantise_lam(2)
        permute_codes(2, 0, 1)
        times_k(0, 0)
        exp_z(1, 0, 0)
        mm_z(2, 0, 0)
        turn_lam(3)
        times_k(0, 1)
        permute_codes(2, 1, 2)
        quantise_conc(0)
        exp_z(1, 1, 0)
        mm_z(2, 0, 1)
        lay_lam(3)
        mm_z(2, 1, 0)
        spread_mass()
        turn_vol()
        quantise_lam(3)
        PERM = {1: 3}
        for f in range(1, len(FRONT) - 1):
            front(turn_lam, f + 3)
            whole(turn_pair, f - 3)
            front(exp_z, f + 1, 0, 0)
            front(mm_z, f + 1, 1, 1)
            back(balance, f - 2, 1)
            back(times_mass, f - 2, 1)
            back(mm_b, f - 1, 0)
            front(exp_z, f + 1, 0, 1)
            front(mm_z, f + 2, 0, 0)
            front(lay_lam, f + 3)
            front(times_k, f, 0)
            front(exp_z, f + 1, 1, 0)
            front(mm_z, f + 2, 0, 1)
            whole(lay_y, f - 3)
            front(times_k, f, 1)
            front(exp_z, f + 1, 1, 1)
            front(mm_z, f + 2, 1, 0)
            back(mm_b, f - 1, 1)
            if f == 1:
                negate_vol()
                copy_mass()
            whole(round_pair, f - 2)
            if f in PERM:
                permute_codes(PERM[f], 0, GROUPS)
            whole(quantise_y, f - 3)
            front(quantise_lam, f + 3)
            back(balance, f - 1, 0)
            front(quantise_conc, f)
            back(times_mass, f - 1, 0)
        store_scales(slice(0, CELLS * 4), nc.sync)
        mm_b(6, 0)
        turn_pair(4)
        times_k(8, 0)
        balance(5, 1)
        quantise_conc(8, 0, 1)
        times_mass(5, 1)
        mm_b(7, 0, 0, 1)
        mm_b(6, 1)
        lay_y(4)
        mm_b(7, 1, 0, 1)
        times_k(8, 1)
        round_pair(5)
        balance(6, 0)
        quantise_conc(8, 1, 2)
        quantise_y(4)
        times_mass(6, 0)
        mm_b(7, 0, 1, 2)
        mm_b(7, 1, 1, 2)
        turn_pair(5)
        lay_y(5)
        balance(6, 1)
        times_mass(6, 1)
        round_y(6, 0)
        balance(7, 0)
        balance(7, 1)
        round_y(6, 1)
        round_y_v(7, 0)
        turn_y(6, 0)
        round_y_v(7, 1)
        turn_y(7, 0)
        turn_y(7, 1)
        turn_y(6, 1)
        lay_y(7)
        times_mass(7, 0)
        times_mass_v(7, 1)
        quantise_y(5)
        lay_y(6)
        quantise_y(7)
        quantise_y(6)
        store_scales(slice(CELLS * 4, CELLS * UNITS), nc.scalar)
